import numpy as np
import ml_dtypes


def mxq(x, axis, fmt="e4m3"):
    dtype, down = {"e4m3": (ml_dtypes.float8_e4m3fn, 7), "e5m2": (ml_dtypes.float8_e5m2, 14)}[fmt]
    v = np.moveaxis(np.asarray(x, np.float32).astype(ml_dtypes.bfloat16).astype(np.float64), axis, -1)
    blocks = v.reshape(v.shape[:-1] + (-1, 32))
    amax = np.abs(blocks).max(-1, keepdims=True)
    byte = np.maximum(np.where(amax > 0, np.frexp(amax)[1] - 1 + 127, 0) - down, 1)
    scale = np.exp2(byte - 127.0)
    codes = (blocks / scale).astype(np.float32).astype(dtype).astype(np.float64)
    return np.moveaxis((codes * scale).reshape(v.shape), -1, axis)


WIDE = False


def mx_kscale(k):
    if not WIDE:
        return np.ones(k)
    levels = np.array([10, -10, 5, -5, 0])
    if k % 512:
        return np.exp2(np.random.permutation(np.resize(levels, k // 32))).repeat(32)
    a = np.empty((k // 512, 16))
    for p in range(k // 512):
        a[p, :8] = np.random.permutation(np.resize(levels, 8))
        for g in range(8):
            far = levels[np.abs(levels - a[p, g]) >= 10]
            a[p, g + 8] = far[np.random.randint(len(far))]
    return np.exp2(a.ravel()).repeat(32)


def f64(x):
    return np.asarray(x).astype(np.float64)


def striped(idx):
    return np.tile(idx.reshape(-1, 16).T, (8, 1)).astype(np.uint16)


def unstriped(offs):
    return offs[:16].T.reshape(-1).astype(np.int64)


E2M1 = np.array([0.0, 0.5, 1.0, 1.5, 2.0, 3.0, 4.0, 6.0, -0.0, -0.5, -1.0, -1.5, -2.0, -3.0, -4.0, -6.0])


def pack_weight(w, fmt):
    k, n = w.shape
    w = f64(np.asarray(w, np.float32).astype(ml_dtypes.bfloat16)).reshape(k // 32, 32, n)
    amax = np.abs(w).max(1)
    if fmt == "e4m3":
        byte = np.frexp(amax)[1] - 1 + 127 - 7
    else:
        mant, ex = np.frexp(amax / 6.0)
        byte = np.where(mant > 0.5, ex, ex - 1) + 127
    byte = np.clip(np.where(amax > 0, byte, 1), 1, 254)
    scaled = (w * np.exp2(127.0 - byte)[:, None, :]).reshape(k, n).astype(np.float32)
    by_word = np.ascontiguousarray(scaled.reshape(k // 512, 128, 4, n).transpose(0, 1, 3, 2))
    if fmt == "e4m3":
        words = by_word.astype(ml_dtypes.float8_e4m3fn).view(np.uint8)
    else:
        c = by_word.astype(ml_dtypes.float4_e2m1fn).view(np.uint8) & 0xF
        words = (c[..., 0::2] | (c[..., 1::2] << 4)).reshape(k // 512, 128, 2 * n)
    return np.ascontiguousarray(words), np.ascontiguousarray(byte.astype(np.uint8).reshape(k // 512, 16, n))


def unpack_weight(words, scales, fmt):
    g, _, n = scales.shape
    words = np.ascontiguousarray(words).reshape(g, 128, n, -1)
    if fmt == "e4m3":
        vals = words.view(ml_dtypes.float8_e4m3fn).astype(np.float64)
    else:
        nib = np.empty((g, 128, n, 4), np.uint8)
        nib[..., 0::2] = words & 0xF
        nib[..., 1::2] = words >> 4
        vals = E2M1[nib]
    vals = vals * np.repeat(np.exp2(scales.astype(np.float64) - 127.0), 8, axis=1)[..., None]
    return vals.transpose(0, 1, 3, 2).reshape(g * 512, n)


def gelu(v):
    return 0.5 * v * (1.0 + np.tanh(np.sqrt(2.0 / np.pi) * (v + 0.044715 * v**3)))


K, H, T, S, T2, P = 1024, 1536, 2048, 512, 1024, 512


def setup_inputs():
    n = np.random.standard_normal
    s = mx_kscale(K)[:, None]
    u = mx_kscale(H)[:, None]
    d = {}
    d["tab_words"], d["tab_scales"] = pack_weight(n((K, T)) * s, "e4m3")
    d["offs"] = striped(np.random.permutation(T)[:S])
    d["w1"] = (n((K, H)) / K ** 0.5 / s * u.T).astype(np.float32)
    d["w4_words"], d["w4_scales"] = pack_weight(n((K, H)) / K ** 0.5 / s * u.T, "e2m1")
    d["res"] = (0.8 * n((H, S)) * u).astype(np.float32)
    d["page0"] = (n((H, T2)) * u).astype(np.float32)
    d["wgs"] = np.exp(0.3 * n((128, S))).astype(np.float32)
    d["offs2"] = striped(np.random.permutation(T2)[:S])
    d["offs3"] = striped(np.random.permutation(T2)[:P])
    d["cen"] = (0.8 * n(H) * u[:, 0]).astype(np.float32)
    d["vec"] = (n(H) / H ** 0.5 / u[:, 0] ** 2).astype(np.float32)
    d["mat"] = np.exp(0.5 * n((T2, P))).astype(np.float32)
    return d


def reference(tab_words, tab_scales, offs, w1, w4_words, w4_scales, res, page0, wgs, offs2, offs3, cen, vec, mat):
    v = unpack_weight(tab_words, tab_scales, "e4m3")[:, unstriped(offs)]
    a1 = mxq(f64(w1), 0, "e4m3").T @ v
    a2 = unpack_weight(w4_words, w4_scales, "e2m1").T @ v
    h = np.maximum(a1, a2) - f64(res)
    page = f64(page0).copy()
    page[:, unstriped(offs2)] = np.tile(f64(wgs), (H // 128, 1)) * h
    x = (page[:, unstriped(offs3)] - f64(cen)[:, None]) * f64(vec)[:, None]
    e = mxq(page, 0, "e4m3").T @ mxq(x, 0, "e4m3")
    return e * f64(mat)

@@ -1,0 +1,354 @@
+from contextlib import ExitStack
+
+import concourse.mybir as mybir
+from concourse.masks import make_identity
+
+F32 = mybir.dt.float32
+BF16 = mybir.dt.bfloat16
+I32 = mybir.dt.int32
+U32 = mybir.dt.uint32
+U16 = mybir.dt.uint16
+U8 = mybir.dt.uint8
+FP8X4 = mybir.dt.float8_e4m3fn_x4
+FP4X4 = mybir.dt.float4_e2m1fn_x4
+ALU = mybir.AluOpType
+ACT = mybir.ActivationFunctionType
+
+K, H, T, S, T2, NP = 1024, 1536, 2048, 512, 1024, 512
+P = 128
+KP = K // 512
+RP = H // 512
+SLICES = H // P
+MT = T2 // P
+W1_CHUNKS = [(c, 1) for c in range(4)] + [(c, 2) for c in range(4, SLICES, 2)]
+VEC_ROW = 32
+FLOPS = 2 * (2 * K * H * S + H * T2 * NP)
+
+
+def tile_list_diamond_master_compare_kernel(
+    tc, tab_words, tab_scales, offs, w1, w4_words, w4_scales, res, page0, wgs, offs2, offs3, cen, vec, mat, out
+):
+    nc = tc.nc
+    with ExitStack() as ctx:
+        lists = ctx.enter_context(tc.tile_pool(name="lists", bufs=1))
+        keep = ctx.enter_context(tc.tile_pool(name="keep", bufs=1))
+        ring = ctx.enter_context(tc.tile_pool(name="ring", bufs=2))
+        psum = ctx.enter_context(tc.psum_pool(name="psum", bufs=1))
+
+        idx = lists.tile([P, S // 16], U16, name="idx")
+        idx2 = lists.tile([P, S // 16], U16, name="idx2")
+        idx3 = lists.tile([P, NP // 16], U16, name="idx3")
+
+        tab_w = [keep.tile([P, T], I32, name="tab_w%d" % a, tag="big%d" % a) for a in range(KP)]
+        tab_s = keep.tile([P, KP, T], U8, name="tab_s", tag="v_w1", align_bytes=64)
+        v_w = {}
+        v_s = [keep.tile([P, S], U8, name="v_s%d" % a, align_bytes=64) for a in range(KP)]
+        w4_w = [keep.tile([P, KP, 1024], U8, name="w4_w%d" % b, align_bytes=64) for b in range(RP)]
+        w4_s = keep.tile([P, KP, H], U8, name="w4_s", align_bytes=64)
+        wg = keep.tile([P, S], F32, name="wg")
+        rows = keep.tile([P, P], F32, name="rows")
+        chan = keep.tile([P, 2 * VEC_ROW], F32, name="chan")
+        shift = keep.tile([P, SLICES], F32, name="shift")
+        warm = keep.tile([P, 8], F32, name="warm")
+        ident32 = keep.tile([P, P], F32, name="ident32")
+        ident16 = keep.tile([P, P], BF16, name="ident16")
+        pg_w = [keep.tile([P, T2], U32, name="pg_w%d" % b, align_bytes=64) for b in range(RP)]
+        pg_s = [keep.tile([P, T2], U8, name="pg_s%d" % b, align_bytes=64) for b in range(RP)]
+        x_w = [keep.tile([P, NP], U32, name="x_w%d" % b, align_bytes=64) for b in range(RP)]
+        x_s = [keep.tile([P, NP], U8, name="x_s%d" % b, align_bytes=64) for b in range(RP)]
+
+        w1_raw, w1_grp, w1_w, w1_s = {}, {}, {}, {}
+        res_t, page, hs, a1_ps, a2_ps, a2_sb, picked, xb, mat_t = {}, {}, {}, {}, {}, {}, {}, {}, {}
+        pg_t, x_t, x_grp, pg_grp, e_ps = {}, {}, {}, {}, {}
+
+        def load_w1(n):
+            first, count = W1_CHUNKS[n]
+            raw = keep.tile([P, KP, 4, P * count], F32, name="w1_raw%d" % n, tag="raw%d" % n)
+            for a in range(KP):
+                src = w1[512 * a : 512 * (a + 1), P * first : P * (first + count)]
+                nc.sync.dma_start(raw[:, a], src.rearrange("(p j) c -> p j c", j=4))
+            for s in range(count):
+                w1_raw[first + s] = raw[:, :, :, P * s : P * (s + 1)]
+
+        def load_table(a):
+            nc.sync.dma_start(tab_w[a][:], tab_words[a].rearrange("p n t -> p (n t)").bitcast(I32))
+
+        def load_w4(b):
+            src = w4_words[:, :, 1024 * b : 1024 * (b + 1)].rearrange("a p c -> p a c")
+            nc.sync.dma_start(w4_w[b][:].bitcast(I32), src.bitcast(I32))
+
+        def load_scale_rows(engine, tile, scale_rows):
+            for q in range(4):
+                src = scale_rows[:, 4 * q : 4 * q + 4, :].rearrange("a r c -> r a c")
+                engine.dma_start(tile[32 * q : 32 * q + 4].bitcast(I32), src.bitcast(I32))
+
+        def load_res(i):
+            res_t[i] = keep.tile([P, S], F32, name="res_t%d" % i)
+            nc.sync.dma_start(res_t[i][:], res[P * i : P * (i + 1), :])
+
+        def load_page(i):
+            page[i] = ring.tile([P, T2], F32, name="page", bufs=8)
+            nc.sync.dma_start(page[i][:], page0[P * i : P * (i + 1), :])
+
+        def load_mat(u):
+            mat_t[u] = keep.tile([P, MT // 2, NP], F32, name="mat_t%d" % u, tag="big%d" % u)
+            nc.sync.dma_start(mat_t[u][:], mat[512 * u : 512 * (u + 1), :].rearrange("(c p) j -> p c j", p=P))
+
+        def round_w1(i):
+            w1_grp[i] = keep.tile([P, KP, P, 4], BF16, name="w1_grp%d" % i, align_bytes=64)
+            nc.scalar.copy(
+                w1_grp[i][:].rearrange("p a (c e) j -> p a c j e", e=4),
+                w1_raw[i].rearrange("p a j (c e) -> p a c j e", e=4),
+            )
+
+        def quantise_w1(i):
+            w1_w[i] = ring.tile([P, KP, P], U32, name="w1_w", bufs=2, align_bytes=64)
+            w1_s[i] = ring.tile([P, KP, P], U8, name="w1_s", bufs=2, align_bytes=64)
+            nc.vector.quantize_mx(
+                w1_w[i][:].rearrange("p a c -> p (a c)").bitcast(FP8X4),
+                w1_s[i][:].rearrange("p a c -> p (a c)"),
+                w1_grp[i][:].rearrange("p a c j -> p (a c j)"),
+            )
+
+        def reading_w1(i):
+            a1_ps[i] = psum.tile([P, S], F32, name="a1", tag="bank_a1")
+            for a in range(KP):
+                nc.tensor.matmul_mx(
+                    a1_ps[i][:], lhsT=w1_w[i][:, a].bitcast(FP8X4), lhsT_scale=w1_s[i][:, a],
+                    rhs=v_w[a][:].bitcast(FP8X4), rhs_scale=v_s[a][:], start=a == 0, stop=a == KP - 1,
+                )
+
+        def reading_w4(i):
+            b, c = divmod(i, 4)
+            a2_ps[i] = psum.tile([P, S], F32, name="a2", tag="bank_a2")
+            for a in range(KP):
+                nc.tensor.matmul_mx(
+                    a2_ps[i][:], lhsT=w4_w[b][:, a, 2 * P * c : 2 * P * (c + 1)].bitcast(FP4X4),
+                    lhsT_scale=w4_s[:, a, P * i : P * (i + 1)],
+                    rhs=v_w[a][:].bitcast(FP8X4), rhs_scale=v_s[a][:], start=a == 0, stop=a == KP - 1,
+                )
+
+        def fetch_w4(i):
+            a2_sb[i] = keep.tile([P, S], F32, name="a2_sb", tag="stage" if i > 0 else "raw0")
+            nc.scalar.copy(a2_sb[i][:], a2_ps[i][:])
+
+        def larger(i):
+            hs[i] = keep.tile([P, S], F32, name="h", tag="h")
+            nc.vector.tensor_tensor(hs[i][:], a1_ps[i][:], a2_sb[i][:], ALU.max)
+
+        def residual(i):
+            nc.vector.tensor_tensor(hs[i][:], hs[i][:], res_t[i][:], ALU.subtract)
+
+        def scatter(i):
+            nc.vector.tensor_tensor(page[i][:].indirect(idx2[:]), hs[i][:], wg[:], ALU.mult)
+
+        def gather(i):
+            picked[i] = keep.tile([P, NP], F32, name="picked", tag="stage")
+            nc.vector.tensor_copy(picked[i][:], page[i][:].indirect(idx3[:]))
+
+        def turn_page(i, tags):
+            b, c = divmod(i, 4)
+            for half in range(2):
+                if c == 0:
+                    pg_t[b, half] = ring.tile([P, 4, 2, 2 * P], BF16, name="pg_t", bufs=4)
+                bank = psum.tile([P, 4, P], F32, name="turn", tag=tags[half])
+                for g in range(4):
+                    m0 = P * (4 * half + g)
+                    nc.tensor.transpose(bank[:, g, :], page[i][:, m0 : m0 + P], ident32[:])
+                nc.scalar.copy(
+                    pg_t[b, half][:, :, :, 64 * c : 64 * (c + 1)].rearrange("m g u (q e) -> m g u q e", e=2),
+                    bank[:].rearrange("m g (q u e) -> m g u q e", u=2, e=2),
+                )
+
+        def centre(i):
+            xb[i] = ring.tile([P, NP], BF16, name="xb", bufs=2)
+            nc.scalar.activation(
+                xb[i][:], picked[i][:], ACT.Identity, bias=shift[:, i : i + 1],
+                scale=chan[:, VEC_ROW + i : VEC_ROW + i + 1],
+            )
+
+        def turn_masters(i, tag, copy):
+            b, c = divmod(i, 4)
+            if c == 0:
+                x_t[b] = ring.tile([P, 4, 2, P], F32, name="x_t", bufs=2)
+            bank = psum.tile([P, 4, P], BF16, name="turn_x", tag=tag)
+            for g in range(4):
+                nc.tensor.transpose(bank[:, g, :], xb[i][:, P * g : P * (g + 1)], ident16[:])
+            copy(
+                x_t[b][:, :, :, 32 * c : 32 * (c + 1)],
+                bank[:].bitcast(F32).rearrange("j g (q u) -> j g u q", u=2),
+            )
+
+        def turn_back(words, dst, tag, copy):
+            bank = psum.tile([P, 2, 2, P], F32, name="back", tag=tag)
+            for g in range(2):
+                for u in range(2):
+                    nc.tensor.transpose(bank[:, g, u, :], words[:, g, u, :], ident32[:])
+            copy(dst.rearrange("p (g m) u -> p g m u", g=2), bank[:].rearrange("p g u m -> p g m u"))
+
+        def finish_masters(b, n, tag, copy):
+            if n == 0:
+                x_grp[b] = ring.tile([P, NP, 2], F32, name="x_grp", bufs=1, align_bytes=64)
+            turn_back(x_t[b][:, 2 * n : 2 * n + 2], x_grp[b][:, 2 * P * n : 2 * P * (n + 1), :], tag, copy)
+
+        def quantise_x(b):
+            nc.vector.quantize_mx(
+                x_w[b][:].bitcast(FP8X4), x_s[b][:], x_grp[b][:].rearrange("p n u -> p (n u)").bitcast(BF16)
+            )
+
+        def finish_page(b, n, tag, copy):
+            pg_grp[b, n] = ring.tile([P, 2 * P, 2], F32, name="pg_grp", bufs=4, align_bytes=64)
+            words = pg_t[b, n // 2][:].bitcast(F32)
+            turn_back(words[:, 2 * (n % 2) : 2 * (n % 2) + 2], pg_grp[b, n][:], tag, copy)
+
+        def quantise_page(b, n):
+            cols = slice(2 * P * n, 2 * P * (n + 1))
+            nc.vector.quantize_mx(
+                pg_w[b][:, cols].bitcast(FP8X4), pg_s[b][:, cols],
+                pg_grp[b, n][:].rearrange("p m u -> p (m u)").bitcast(BF16),
+            )
+
+        e_banks = ["bank_e0", "bank_e1", "bank_e2", "bank_a1", "bank_a2", "bank_t0", "bank_t1", "bank_w"]
+
+        def scores(m, b):
+            if b == 0:
+                e_ps[m] = psum.tile([P, NP], F32, name="e_ps", tag=e_banks[m])
+            cols = slice(P * m, P * (m + 1))
+            nc.tensor.matmul_mx(
+                e_ps[m][:], lhsT=pg_w[b][:, cols].bitcast(FP8X4), lhsT_scale=pg_s[b][:, cols],
+                rhs=x_w[b][:].bitcast(FP8X4), rhs_scale=x_s[b][:], start=b == 0, stop=b == RP - 1,
+            )
+
+        def weigh(m):
+            result = keep.tile([P, NP], F32, name="result", tag="raw%d" % (m % len(W1_CHUNKS)))
+            nc.vector.tensor_tensor(result[:], e_ps[m][:], mat_t[m // 4][:, m % 4, :], ALU.mult)
+            nc.sync.dma_start(out[P * m : P * (m + 1), :], result[:])
+
+        nc.vector.memset(tab_s[:].bitcast(I32), 0)
+        nc.vector.memset(warm[:], 0.0)
+        nc.scalar.activation(warm[:, 0:1], warm[:, 1:2], ACT.Identity, bias=warm[:, 2:3], scale=warm[:, 3:4])
+        nc.gpsimd.memset(w4_s[:].bitcast(I32), 0)
+        load_scale_rows(nc.gpsimd, w4_s, w4_scales)
+        make_identity(nc, ident32[:])
+        nc.gpsimd.memset(rows[:], 0.0)
+        make_identity(nc, ident16[:])
+
+        nc.sync.dma_start(idx[:], offs)
+        load_table(0)
+        load_scale_rows(nc.sync, tab_s, tab_scales)
+        load_table(1)
+        load_w1(0)
+        load_w4(0)
+        load_w1(1)
+        load_res(0)
+        nc.sync.dma_start(wg[:], wgs)
+        nc.sync.dma_start(idx2[:], offs2)
+        load_page(0)
+        load_w1(2)
+        nc.sync.dma_start(idx3[:], offs3)
+        nc.sync.dma_start(rows[0:SLICES, :], cen.rearrange("(c p) -> c p", p=P))
+        nc.sync.dma_start(rows[VEC_ROW : VEC_ROW + SLICES, :], vec.rearrange("(c p) -> c p", p=P))
+        load_res(1)
+        for i in range(1, SLICES - 1):
+            if i + 2 < len(W1_CHUNKS):
+                load_w1(i + 2)
+            load_res(i + 1)
+            if i % 4 == 2 and i // 4 + 1 < RP:
+                load_w4(i // 4 + 1)
+            load_page(i)
+        for u in range(2):
+            load_mat(u)
+
+        for a in range(KP):
+            nc.vector.tensor_copy(v_s[a][:], tab_s[:, a, :].indirect(idx[:]))
+        for a in range(KP):
+            v_w[a] = keep.tile([P, S], U32, name="v_w%d" % a, tag="v_w%d" % a, align_bytes=64)
+            nc.vector.tensor_copy(v_w[a][:], tab_w[a][:].bitcast(U32).indirect(idx[:]))
+        reading_w4(0)
+        round_w1(0)
+        quantise_w1(0)
+        fetch_w4(0)
+        reading_w1(0)
+        round_w1(1)
+        larger(0)
+        reading_w4(1)
+        quantise_w1(1)
+        residual(0)
+        fetch_w4(1)
+        reading_w1(1)
+        turned = psum.tile([P, P], F32, name="turned", tag="bank_w")
+        nc.tensor.transpose(turned[:], rows[:], ident32[:])
+        nc.scalar.copy(chan[:], turned[:, 0 : 2 * VEC_ROW])
+        round_w1(2)
+        nc.vector.scalar_tensor_tensor(
+            shift[:], chan[:, 0:SLICES], -1.0, chan[:, VEC_ROW : VEC_ROW + SLICES], ALU.mult, ALU.mult
+        )
+        round_w1(3)
+        quantise_w1(2)
+        round_w1(4)
+
+        last = RP - 1
+        for i in range(SLICES - 1):
+            b, c = divmod(i, 4)
+            scatter(i)
+            larger(i + 1)
+            turn_page(i, ["bank_t0", "bank_a2" if i + 2 < SLICES else "bank_t1"])
+            if i + 2 < SLICES:
+                reading_w1(i + 2)
+                reading_w4(i + 2)
+            gather(i)
+            residual(i + 1)
+            if i + 3 < SLICES:
+                quantise_w1(i + 3)
+            centre(i)
+            if i + 2 < SLICES:
+                fetch_w4(i + 2)
+            turn_masters(i, "bank_t0", nc.scalar.copy)
+            if b > 0 and c == 0:
+                finish_masters(b - 1, 0, "bank_w", nc.scalar.copy)
+                finish_masters(b - 1, 1, "bank_t1", nc.scalar.copy)
+                quantise_x(b - 1)
+            first = 2 * (c - 1) if b < last else 2 * c
+            if b > 0 and 0 <= first < 4:
+                for n, tag in ((first, "bank_w"), (first + 1, "bank_t1")):
+                    finish_page(b - 1, n, tag, nc.scalar.copy)
+                    quantise_page(b - 1, n)
+            if i + 5 < SLICES:
+                round_w1(i + 5)
+            if i == 7:
+                for m in range(3):
+                    scores(m, 0)
+            if i == SLICES - 2:
+                for m in range(3):
+                    scores(m, 1)
+                for m in range(3, 5):
+                    for bb in range(last):
+                        scores(m, bb)
+            if i == 3:
+                load_page(SLICES - 1)
+
+        i = SLICES - 1
+        scatter(i)
+        turn_page(i, ["bank_t0", "bank_t1"])
+        gather(i)
+        xb[i] = ring.tile([P, NP], BF16, name="xb", bufs=2)
+        nc.vector.tensor_scalar(
+            xb[i][:], picked[i][:], chan[:, i : i + 1], chan[:, VEC_ROW + i : VEC_ROW + i + 1], ALU.subtract, ALU.mult
+        )
+        finish_page(last, 0, "bank_w", nc.scalar.copy)
+        turn_masters(i, "bank_t0", nc.vector.tensor_copy)
+        finish_page(last, 1, "bank_t1", nc.scalar.copy)
+        finish_masters(last, 0, "bank_w", nc.scalar.copy)
+        finish_masters(last, 1, "bank_t0", nc.vector.tensor_copy)
+        quantise_page(last, 0)
+        quantise_x(last)
+        finish_page(last, 2, "bank_t1", nc.scalar.copy)
+        finish_page(last, 3, "bank_w", nc.scalar.copy)
+        for m in range(MT):
+            if m % 2 == 1 and m < MT - 1:
+                quantise_page(last, (m + 1) // 2)
+            if m >= 5:
+                for bb in range(last):
+                    scores(m, bb)
+            scores(m, last)
+            weigh(m)

@@ -1,7 +1,6 @@
 from contextlib import ExitStack
 
 import concourse.mybir as mybir
-from concourse.masks import make_identity
 
 F32 = mybir.dt.float32
 BF16 = mybir.dt.bfloat16
@@ -20,7 +19,8 @@ KP = K // 512
 RP = H // 512
 SLICES = H // P
 MT = T2 // P
-W1_CHUNKS = [(c, 1) for c in range(4)] + [(c, 2) for c in range(4, SLICES, 2)]
+TURNED = SLICES - 4
+W1_CHUNKS = [(c, 1) for c in range(4)] + [(c, 2) for c in range(4, TURNED, 2)]
 VEC_ROW = 32
 FLOPS = 2 * (2 * K * H * S + H * T2 * NP)
 
@@ -31,16 +31,42 @@ def tile_list_diamond_master_compare_kernel(
     nc = tc.nc
     with ExitStack() as ctx:
         lists = ctx.enter_context(tc.tile_pool(name="lists", bufs=1))
-        keep = ctx.enter_context(tc.tile_pool(name="keep", bufs=1))
-        ring = ctx.enter_context(tc.tile_pool(name="ring", bufs=2))
+        first = ctx.enter_context(tc.tile_pool(name="first", bufs=1))
         psum = ctx.enter_context(tc.psum_pool(name="psum", bufs=1))
 
         idx = lists.tile([P, S // 16], U16, name="idx")
         idx2 = lists.tile([P, S // 16], U16, name="idx2")
         idx3 = lists.tile([P, NP // 16], U16, name="idx3")
 
-        tab_w = [keep.tile([P, T], I32, name="tab_w%d" % a, tag="big%d" % a) for a in range(KP)]
-        tab_s = keep.tile([P, KP, T], U8, name="tab_s", tag="v_w1", align_bytes=64)
+        tab_w, mat_t = {}, {}
+        tab_w[0] = first.tile([P, T], I32, name="tab_w0", tag="big0")
+        tab_s = first.tile([P, KP, T], U8, name="tab_s", tag="v_w1", align_bytes=64)
+        warm = first.tile([P, 8], F32, name="warm")
+        ident32 = first.tile([P, P], F32, name="ident32")
+        ident16 = first.tile([P, P], BF16, name="ident16")
+
+        def load_table(a):
+            nc.sync.dma_start(tab_w[a][:], tab_words[a].rearrange("p n t -> p (n t)").bitcast(I32))
+
+        def load_scale_rows(tile, scale_rows):
+            for q in range(4):
+                src = scale_rows[:, 4 * q : 4 * q + 4, :].rearrange("a r c -> r a c")
+                nc.sync.dma_start(tile[32 * q : 32 * q + 4].bitcast(I32), src.bitcast(I32))
+
+        nc.sync.dma_start(idx[:], offs)
+        load_table(0)
+        nc.vector.memset(tab_s[:].bitcast(I32), 0)
+        load_scale_rows(tab_s, tab_scales)
+        with tc.tile_pool(name="scratch", bufs=1) as scratch:
+            ones = scratch.tile([P, P], F32, name="ones")
+            nc.vector.memset(ones[:], 1.0)
+            nc.gpsimd.affine_select(
+                out=ident32[:], in_=ones[:], compare_op=ALU.is_equal, fill=0.0, base=0,
+                pattern=[[-1, P]], channel_multiplier=1,
+            )
+
+        keep = ctx.enter_context(tc.tile_pool(name="keep", bufs=1))
+        tab_w[1] = keep.tile([P, T], I32, name="tab_w1", tag="big1")
         v_w = {}
         v_s = [keep.tile([P, S], U8, name="v_s%d" % a, align_bytes=64) for a in range(KP)]
         w4_w = [keep.tile([P, KP, 1024], U8, name="w4_w%d" % b, align_bytes=64) for b in range(RP)]
@@ -48,67 +74,100 @@ def tile_list_diamond_master_compare_kernel(
         wg = keep.tile([P, S], F32, name="wg")
         rows = keep.tile([P, P], F32, name="rows")
         chan = keep.tile([P, 2 * VEC_ROW], F32, name="chan")
-        shift = keep.tile([P, SLICES], F32, name="shift")
-        warm = keep.tile([P, 8], F32, name="warm")
-        ident32 = keep.tile([P, P], F32, name="ident32")
-        ident16 = keep.tile([P, P], BF16, name="ident16")
+        shift = keep.tile([P, TURNED], F32, name="shift")
+        raw_d = keep.tile([P, KP, 4, 512], F32, name="raw_d", align_bytes=64)
+        dealt, top = {}, {}
+        wg_d = keep.tile([P, 4, S], F32, name="wg_d")
+        cen_d = keep.tile([P, 4], F32, name="cen_d")
+        vec_d = keep.tile([P, 4], F32, name="vec_d")
+        shift_d = keep.tile([P, 4], F32, name="shift_d")
+        x_d = keep.tile([P, NP, 4], BF16, name="x_d", align_bytes=64)
         pg_w = [keep.tile([P, T2], U32, name="pg_w%d" % b, align_bytes=64) for b in range(RP)]
         pg_s = [keep.tile([P, T2], U8, name="pg_s%d" % b, align_bytes=64) for b in range(RP)]
         x_w = [keep.tile([P, NP], U32, name="x_w%d" % b, align_bytes=64) for b in range(RP)]
         x_s = [keep.tile([P, NP], U8, name="x_s%d" % b, align_bytes=64) for b in range(RP)]
 
         w1_raw, w1_grp, w1_w, w1_s = {}, {}, {}, {}
-        res_t, page, hs, a1_ps, a2_ps, a2_sb, picked, xb, mat_t = {}, {}, {}, {}, {}, {}, {}, {}, {}
-        pg_t, x_t, x_grp, pg_grp, e_ps = {}, {}, {}, {}, {}
+        res_t, page, hs, a1_ps, a2_ps, a2_sb, picked, xb = {}, {}, {}, {}, {}, {}, {}, {}
+        pg_t, x_t, x_grp, pg_grp, e_ps, pairs = {}, {}, {}, {}, {}, {}
 
         def load_w1(n):
             first, count = W1_CHUNKS[n]
-            raw = keep.tile([P, KP, 4, P * count], F32, name="w1_raw%d" % n, tag="raw%d" % n)
+            raw = keep.tile([P, KP, 4, P * count], F32, name="w1_raw%d" % n, tag="raw%d" % n, align_bytes=64)
             for a in range(KP):
                 src = w1[512 * a : 512 * (a + 1), P * first : P * (first + count)]
                 nc.sync.dma_start(raw[:, a], src.rearrange("(p j) c -> p j c", j=4))
             for s in range(count):
                 w1_raw[first + s] = raw[:, :, :, P * s : P * (s + 1)]
 
-        def load_table(a):
-            nc.sync.dma_start(tab_w[a][:], tab_words[a].rearrange("p n t -> p (n t)").bitcast(I32))
+        def rows_of(i):
+            if i < TURNED:
+                return slice(P * i, P * (i + 1))
+            return slice(P * TURNED + i - TURNED, H, 4)
+
+        def load_w1_dealt(a):
+            src = w1[512 * a : 512 * (a + 1), P * TURNED :]
+            nc.sync.dma_start(raw_d[:, a], src.rearrange("(p j) c -> p j c", j=4))
 
         def load_w4(b):
             src = w4_words[:, :, 1024 * b : 1024 * (b + 1)].rearrange("a p c -> p a c")
             nc.sync.dma_start(w4_w[b][:].bitcast(I32), src.bitcast(I32))
 
-        def load_scale_rows(engine, tile, scale_rows):
-            for q in range(4):
-                src = scale_rows[:, 4 * q : 4 * q + 4, :].rearrange("a r c -> r a c")
-                engine.dma_start(tile[32 * q : 32 * q + 4].bitcast(I32), src.bitcast(I32))
-
         def load_res(i):
-            res_t[i] = keep.tile([P, S], F32, name="res_t%d" % i)
-            nc.sync.dma_start(res_t[i][:], res[P * i : P * (i + 1), :])
+            res_t[i] = keep.tile([P, S], F32, name="res_t", tag="res%d" % i, align_bytes=64)
+            nc.sync.dma_start(res_t[i][:], res[rows_of(i), :])
 
         def load_page(i):
-            page[i] = ring.tile([P, T2], F32, name="page", bufs=8)
-            nc.sync.dma_start(page[i][:], page0[P * i : P * (i + 1), :])
+            page[i] = keep.tile([P, T2], F32, name="page", bufs=8)
+            nc.sync.dma_start(page[i][:], page0[rows_of(i), :])
 
         def load_mat(u):
-            mat_t[u] = keep.tile([P, MT // 2, NP], F32, name="mat_t%d" % u, tag="big%d" % u)
+            mat_t[u] = (first, keep)[u].tile([P, MT // 2, NP], F32, name="mat_t%d" % u, tag="big%d" % u)
             nc.sync.dma_start(mat_t[u][:], mat[512 * u : 512 * (u + 1), :].rearrange("(c p) j -> p c j", p=P))
 
-        def round_w1(i):
-            w1_grp[i] = keep.tile([P, KP, P, 4], BF16, name="w1_grp%d" % i, align_bytes=64)
+        def round_w1(i, parts=1):
+            tag = "w1q%d" % ((i - 2) % 3) if i > 0 else "grp0"
+            grp = keep.tile([P, KP, P, 4], BF16, name="w1_grp", tag=tag, align_bytes=64)
+            w1_grp[i] = grp[:]
+            for a0 in range(0, KP, KP // parts):
+                passes = slice(a0, a0 + KP // parts)
+                nc.scalar.copy(
+                    w1_grp[i][:, passes].rearrange("p a (c e) j -> p a c j e", e=4),
+                    w1_raw[i][:, passes].rearrange("p a j (c e) -> p a c j e", e=4),
+                )
+
+        def round_w1_dealt(n):
+            a, half = divmod(n, 2)
+            if n == 0:
+                dealt["w1"] = keep.tile([P, 4, KP, P, 4], BF16, name="grp_d", tag="raw4", align_bytes=64)
             nc.scalar.copy(
-                w1_grp[i][:].rearrange("p a (c e) j -> p a c j e", e=4),
-                w1_raw[i].rearrange("p a j (c e) -> p a c j e", e=4),
+                dealt["w1"][:, :, a, 64 * half : 64 * (half + 1), :].rearrange("p t q j -> p q j t"),
+                raw_d[:, a, :, 256 * half : 256 * (half + 1)].rearrange("p j (q t) -> p q j t", t=4),
             )
 
-        def quantise_w1(i):
-            w1_w[i] = ring.tile([P, KP, P], U32, name="w1_w", bufs=2, align_bytes=64)
-            w1_s[i] = ring.tile([P, KP, P], U8, name="w1_s", bufs=2, align_bytes=64)
-            nc.vector.quantize_mx(
-                w1_w[i][:].rearrange("p a c -> p (a c)").bitcast(FP8X4),
-                w1_s[i][:].rearrange("p a c -> p (a c)"),
-                w1_grp[i][:].rearrange("p a c j -> p (a c j)"),
-            )
+        def deal_w4_words():
+            dealt["words"] = keep.tile([P, 4, KP, 2 * P], U8, name="w4_wd", tag="grp0", align_bytes=64)
+            last_block = w4_w[RP - 1][:].bitcast(U16).rearrange("p a (q t) -> p t a q", t=4)
+            nc.vector.tensor_copy(dealt["words"][:].bitcast(U16), last_block)
+
+        def deal_w4_scales():
+            dealt["scales"] = keep.tile([P, 4, KP, P], U8, name="w4_sd", tag="raw0", align_bytes=64)
+            last_block = w4_s[:, :, P * TURNED :].rearrange("p a (q t) -> p t a q", t=4)
+            nc.vector.tensor_copy(dealt["scales"][:], last_block)
+
+        def quantise_w1(i, parts=1):
+            plane_tag = "w1_s%d" % i if i < 2 else "res%d" % (i - 1 if i < 4 else i - 2)
+            w1_w[i] = keep.tile([P, KP, P], U32, name="w1_w", tag="w1q%d" % (i % 3), align_bytes=64)
+            w1_s[i] = keep.tile([P, KP, P], U8, name="w1_s", tag=plane_tag, align_bytes=64)
+            if i >= TURNED:
+                w1_grp[i] = dealt["w1"][:, i - TURNED]
+            for a0 in range(0, KP, KP // parts):
+                passes = slice(a0, a0 + KP // parts)
+                nc.vector.quantize_mx(
+                    w1_w[i][:, passes].rearrange("p a c -> p (a c)").bitcast(FP8X4),
+                    w1_s[i][:, passes].rearrange("p a c -> p (a c)"),
+                    w1_grp[i][:, passes].rearrange("p a c j -> p (a c j)"),
+                )
 
         def reading_w1(i):
             a1_ps[i] = psum.tile([P, S], F32, name="a1", tag="bank_a1")
@@ -122,35 +181,41 @@ def tile_list_diamond_master_compare_kernel(
             b, c = divmod(i, 4)
             a2_ps[i] = psum.tile([P, S], F32, name="a2", tag="bank_a2")
             for a in range(KP):
+                if i < TURNED:
+                    words, scales = w4_w[b][:, a, 2 * P * c : 2 * P * (c + 1)], w4_s[:, a, P * i : P * (i + 1)]
+                else:
+                    words, scales = dealt["words"][:, c, a], dealt["scales"][:, c, a]
                 nc.tensor.matmul_mx(
-                    a2_ps[i][:], lhsT=w4_w[b][:, a, 2 * P * c : 2 * P * (c + 1)].bitcast(FP4X4),
-                    lhsT_scale=w4_s[:, a, P * i : P * (i + 1)],
+                    a2_ps[i][:], lhsT=words.bitcast(FP4X4), lhsT_scale=scales,
                     rhs=v_w[a][:].bitcast(FP8X4), rhs_scale=v_s[a][:], start=a == 0, stop=a == KP - 1,
                 )
 
         def fetch_w4(i):
-            a2_sb[i] = keep.tile([P, S], F32, name="a2_sb", tag="stage" if i > 0 else "raw0")
+            a2_sb[i] = keep.tile([P, S], F32, name="a2_sb", tag="raw1" if i > 0 else "raw0", align_bytes=64)
             nc.scalar.copy(a2_sb[i][:], a2_ps[i][:])
 
         def larger(i):
-            hs[i] = keep.tile([P, S], F32, name="h", tag="h")
-            nc.vector.tensor_tensor(hs[i][:], a1_ps[i][:], a2_sb[i][:], ALU.max)
+            top[i] = keep.tile([P, S], F32, name="top", tag="top" if i != 1 else "h0")
+            nc.vector.tensor_tensor(top[i][:], a1_ps[i][:], a2_sb[i][:], ALU.max)
 
         def residual(i):
-            nc.vector.tensor_tensor(hs[i][:], hs[i][:], res_t[i][:], ALU.subtract)
+            hs[i] = keep.tile([P, S], F32, name="h", tag="h%d" % (i % 2))
+            engine = nc.gpsimd if i > 0 else nc.vector
+            engine.tensor_tensor(hs[i][:], top[i][:], res_t[i][:], ALU.subtract)
 
         def scatter(i):
-            nc.vector.tensor_tensor(page[i][:].indirect(idx2[:]), hs[i][:], wg[:], ALU.mult)
+            nc.vector.tensor_tensor(page[i][:].indirect(idx2[:]), hs[i][:], wg[:] if i < TURNED else wg_d[:, i - TURNED], ALU.mult)
 
         def gather(i):
-            picked[i] = keep.tile([P, NP], F32, name="picked", tag="stage")
+            picked[i] = keep.tile([P, NP], F32, name="picked", tag="raw1", align_bytes=64)
             nc.vector.tensor_copy(picked[i][:], page[i][:].indirect(idx3[:]))
 
         def turn_page(i, tags):
             b, c = divmod(i, 4)
             for half in range(2):
                 if c == 0:
-                    pg_t[b, half] = ring.tile([P, 4, 2, 2 * P], BF16, name="pg_t", bufs=4)
+                    tag = "raw2" if (b, half) == (0, 0) else "pg_t%d%d" % (b, half)
+                    pg_t[b, half] = keep.tile([P, 4, 2, 2 * P], BF16, name="pg_t", tag=tag, align_bytes=64)
                 bank = psum.tile([P, 4, P], F32, name="turn", tag=tags[half])
                 for g in range(4):
                     m0 = P * (4 * half + g)
@@ -160,24 +225,49 @@ def tile_list_diamond_master_compare_kernel(
                     bank[:].rearrange("m g (q u e) -> m g u q e", u=2, e=2),
                 )
 
+        def negated_product(dst, left, right):
+            nc.gpsimd.tensor_tensor(dst, left, right, ALU.mult)
+            nc.gpsimd.tensor_scalar(dst, dst, -1.0, 0.0, ALU.mult, ALU.add)
+
         def centre(i):
-            xb[i] = ring.tile([P, NP], BF16, name="xb", bufs=2)
+            if i < TURNED - 1:
+                xb[i] = keep.tile([P, NP], BF16, name="xb", bufs=2)
+            else:
+                xb[i] = keep.tile([P, NP], BF16, name="xb_last", tag="raw5", align_bytes=64)
             nc.scalar.activation(
                 xb[i][:], picked[i][:], ACT.Identity, bias=shift[:, i : i + 1],
                 scale=chan[:, VEC_ROW + i : VEC_ROW + i + 1],
             )
 
-        def turn_masters(i, tag, copy):
+        def round_page(i, c0, c1):
+            u, e = divmod(i - TURNED, 2)
+            nc.scalar.copy(pairs[0][:, u, c0:c1, e], page[i][:, c0:c1])
+
+        def weave_page(n):
+            pg_grp[RP - 1, n] = keep.tile([P, 2 * P, 2], F32, name="pg_grp", bufs=4, align_bytes=64)
+            words = pairs[0][:].rearrange("p u m e -> p u (m e)").bitcast(F32)
+            nc.scalar.copy(pg_grp[RP - 1, n][:], words[:, :, 2 * P * n : 2 * P * (n + 1)].rearrange("p u m -> p m u"))
+
+        def centre_dealt(i):
+            t = i - TURNED
+            nc.scalar.activation(
+                x_d[:, :, t], picked[i][:], ACT.Identity, bias=shift_d[:, t : t + 1], scale=vec_d[:, t : t + 1]
+            )
+
+        def turn_masters(i, tags, copy):
             b, c = divmod(i, 4)
             if c == 0:
-                x_t[b] = ring.tile([P, 4, 2, P], F32, name="x_t", bufs=2)
-            bank = psum.tile([P, 4, P], BF16, name="turn_x", tag=tag)
-            for g in range(4):
-                nc.tensor.transpose(bank[:, g, :], xb[i][:, P * g : P * (g + 1)], ident16[:])
-            copy(
-                x_t[b][:, :, :, 32 * c : 32 * (c + 1)],
-                bank[:].bitcast(F32).rearrange("j g (q u) -> j g u q", u=2),
-            )
+                x_t[b] = keep.tile([P, 4, 2, P], F32, name="x_t", bufs=2)
+            share = 4 // len(tags)
+            for n, tag in enumerate(tags):
+                bank = psum.tile([P, share, P], BF16, name="turn_x", tag=tag)
+                for g in range(share):
+                    j0 = P * (share * n + g)
+                    nc.tensor.transpose(bank[:, g, :], xb[i][:, j0 : j0 + P], ident16[:])
+                copy(
+                    x_t[b][:, share * n : share * (n + 1), :, 32 * c : 32 * (c + 1)],
+                    bank[:].bitcast(F32).rearrange("j g (q u) -> j g u q", u=2),
+                )
 
         def turn_back(words, dst, tag, copy):
             bank = psum.tile([P, 2, 2, P], F32, name="back", tag=tag)
@@ -188,27 +278,27 @@ def tile_list_diamond_master_compare_kernel(
 
         def finish_masters(b, n, tag, copy):
             if n == 0:
-                x_grp[b] = ring.tile([P, NP, 2], F32, name="x_grp", bufs=1, align_bytes=64)
+                x_grp[b] = keep.tile([P, NP, 2], F32, name="x_grp", bufs=1, align_bytes=64)
             turn_back(x_t[b][:, 2 * n : 2 * n + 2], x_grp[b][:, 2 * P * n : 2 * P * (n + 1), :], tag, copy)
 
         def quantise_x(b):
-            nc.vector.quantize_mx(
-                x_w[b][:].bitcast(FP8X4), x_s[b][:], x_grp[b][:].rearrange("p n u -> p (n u)").bitcast(BF16)
-            )
+            if b < RP - 1:
+                src = x_grp[b][:].rearrange("p n u -> p (n u)").bitcast(BF16)
+            else:
+                src = x_d[:].rearrange("p n t -> p (n t)")
+            nc.vector.quantize_mx(x_w[b][:].bitcast(FP8X4), x_s[b][:], src)
 
         def finish_page(b, n, tag, copy):
-            pg_grp[b, n] = ring.tile([P, 2 * P, 2], F32, name="pg_grp", bufs=4, align_bytes=64)
+            pg_grp[b, n] = keep.tile([P, 2 * P, 2], F32, name="pg_grp", bufs=4, align_bytes=64)
             words = pg_t[b, n // 2][:].bitcast(F32)
             turn_back(words[:, 2 * (n % 2) : 2 * (n % 2) + 2], pg_grp[b, n][:], tag, copy)
 
         def quantise_page(b, n):
             cols = slice(2 * P * n, 2 * P * (n + 1))
-            nc.vector.quantize_mx(
-                pg_w[b][:, cols].bitcast(FP8X4), pg_s[b][:, cols],
-                pg_grp[b, n][:].rearrange("p m u -> p (m u)").bitcast(BF16),
-            )
+            src = pg_grp[b, n][:].rearrange("p m u -> p (m u)").bitcast(BF16)
+            nc.vector.quantize_mx(pg_w[b][:, cols].bitcast(FP8X4), pg_s[b][:, cols], src)
 
-        e_banks = ["bank_e0", "bank_e1", "bank_e2", "bank_a1", "bank_a2", "bank_t0", "bank_t1", "bank_w"]
+        e_banks = ["bank_e0", "bank_e1", "bank_t0", "bank_t1", "bank_a2", "bank_a1", "bank_w0", "bank_w1"]
 
         def scores(m, b):
             if b == 0:
@@ -219,136 +309,143 @@ def tile_list_diamond_master_compare_kernel(
                 rhs=x_w[b][:].bitcast(FP8X4), rhs_scale=x_s[b][:], start=b == 0, stop=b == RP - 1,
             )
 
+        result_tags = ["res%d" % m for m in range(MT)]
+
         def weigh(m):
-            result = keep.tile([P, NP], F32, name="result", tag="raw%d" % (m % len(W1_CHUNKS)))
+            result = keep.tile([P, NP], F32, name="result", tag=result_tags[m], align_bytes=64)
             nc.vector.tensor_tensor(result[:], e_ps[m][:], mat_t[m // 4][:, m % 4, :], ALU.mult)
             nc.sync.dma_start(out[P * m : P * (m + 1), :], result[:])
 
-        nc.vector.memset(tab_s[:].bitcast(I32), 0)
         nc.vector.memset(warm[:], 0.0)
         nc.scalar.activation(warm[:, 0:1], warm[:, 1:2], ACT.Identity, bias=warm[:, 2:3], scale=warm[:, 3:4])
         nc.gpsimd.memset(w4_s[:].bitcast(I32), 0)
-        load_scale_rows(nc.gpsimd, w4_s, w4_scales)
-        make_identity(nc, ident32[:])
         nc.gpsimd.memset(rows[:], 0.0)
-        make_identity(nc, ident16[:])
+        nc.gpsimd.tensor_copy(ident16[:], ident32[:])
 
-        nc.sync.dma_start(idx[:], offs)
-        load_table(0)
-        load_scale_rows(nc.sync, tab_s, tab_scales)
         load_table(1)
-        load_w1(0)
         load_w4(0)
+        load_scale_rows(w4_s, w4_scales)
+        load_w4(RP - 1)
+        load_w1(0)
         load_w1(1)
-        load_res(0)
         nc.sync.dma_start(wg[:], wgs)
         nc.sync.dma_start(idx2[:], offs2)
         load_page(0)
+        load_res(0)
         load_w1(2)
         nc.sync.dma_start(idx3[:], offs3)
-        nc.sync.dma_start(rows[0:SLICES, :], cen.rearrange("(c p) -> c p", p=P))
-        nc.sync.dma_start(rows[VEC_ROW : VEC_ROW + SLICES, :], vec.rearrange("(c p) -> c p", p=P))
-        load_res(1)
-        for i in range(1, SLICES - 1):
-            if i + 2 < len(W1_CHUNKS):
-                load_w1(i + 2)
-            load_res(i + 1)
-            if i % 4 == 2 and i // 4 + 1 < RP:
-                load_w4(i // 4 + 1)
+        nc.sync.dma_start(rows[0:TURNED, :], cen[: P * TURNED].rearrange("(c p) -> c p", p=P))
+        nc.sync.dma_start(rows[VEC_ROW : VEC_ROW + TURNED, :], vec[: P * TURNED].rearrange("(c p) -> c p", p=P))
+        nc.sync.dma_start(cen_d[:], cen[P * TURNED :].rearrange("(p t) -> p t", t=4))
+        nc.sync.dma_start(vec_d[:], vec[P * TURNED :].rearrange("(p t) -> p t", t=4))
+        w1_before = {1: (3, 4), 2: (5,)}
+        for i in range(1, SLICES):
+            for n in w1_before.get(i, ()):
+                load_w1(n)
+            if i == 2:
+                load_w4(1)
+            if 0 <= i - 3 < KP:
+                load_w1_dealt(i - 3)
+            if i == TURNED:
+                for u in range(4):
+                    nc.sync.dma_start(wg_d[32 * u : 32 * (u + 1)], wgs.rearrange("(q t) j -> q t j", t=4))
             load_page(i)
+            load_res(i)
         for u in range(2):
             load_mat(u)
 
         for a in range(KP):
             nc.vector.tensor_copy(v_s[a][:], tab_s[:, a, :].indirect(idx[:]))
         for a in range(KP):
-            v_w[a] = keep.tile([P, S], U32, name="v_w%d" % a, tag="v_w%d" % a, align_bytes=64)
+            v_w[a] = first.tile([P, S], U32, name="v_w%d" % a, tag="v_w%d" % a, align_bytes=64)
             nc.vector.tensor_copy(v_w[a][:], tab_w[a][:].bitcast(U32).indirect(idx[:]))
         reading_w4(0)
-        round_w1(0)
-        quantise_w1(0)
+        round_w1(0, KP)
+        quantise_w1(0, KP)
         fetch_w4(0)
         reading_w1(0)
+        deal_w4_words()
         round_w1(1)
         larger(0)
+        deal_w4_scales()
         reading_w4(1)
         quantise_w1(1)
         residual(0)
         fetch_w4(1)
         reading_w1(1)
-        turned = psum.tile([P, P], F32, name="turned", tag="bank_w")
+        reading_w4(2)
+        turned = psum.tile([P, P], F32, name="turned", tag="bank_w0")
         nc.tensor.transpose(turned[:], rows[:], ident32[:])
         nc.scalar.copy(chan[:], turned[:, 0 : 2 * VEC_ROW])
         round_w1(2)
-        nc.vector.scalar_tensor_tensor(
-            shift[:], chan[:, 0:SLICES], -1.0, chan[:, VEC_ROW : VEC_ROW + SLICES], ALU.mult, ALU.mult
-        )
+        negated_product(shift[:], chan[:, 0:TURNED], chan[:, VEC_ROW : VEC_ROW + TURNED])
         round_w1(3)
-        quantise_w1(2)
-        round_w1(4)
+
+        negated_product(shift_d[:], cen_d[:], vec_d[:])
 
         last = RP - 1
+        page_parts = {5: (0, 1), 6: (2, 3), 8: (0,), 9: (1, 2, 3)}
         for i in range(SLICES - 1):
             b, c = divmod(i, 4)
             scatter(i)
             larger(i + 1)
-            turn_page(i, ["bank_t0", "bank_a2" if i + 2 < SLICES else "bank_t1"])
-            if i + 2 < SLICES:
+            if 2 <= i < SLICES - 2:
                 reading_w1(i + 2)
-                reading_w4(i + 2)
+            if i < TURNED:
+                turn_page(i, ["bank_t0", "bank_t1"])
+            else:
+                if i == TURNED:
+                    pairs[0] = keep.tile([P, 2, T2, 2], BF16, name="pairs", tag="raw5", align_bytes=64)
+                round_page(i, 0, T2 // 2)
             gather(i)
             residual(i + 1)
-            if i + 3 < SLICES:
+            if i < 2:
+                quantise_w1(i + 2)
+                reading_w1(i + 2)
+            if 1 <= i < SLICES - 3:
                 quantise_w1(i + 3)
-            centre(i)
+            if i < TURNED:
+                centre(i)
+            else:
+                centre_dealt(i)
             if i + 2 < SLICES:
                 fetch_w4(i + 2)
-            turn_masters(i, "bank_t0", nc.scalar.copy)
+            if i + 3 < SLICES:
+                reading_w4(i + 3)
+            if i < TURNED - 1:
+                turn_masters(i, ["bank_t0", "bank_t1"], nc.scalar.copy)
+            if i == TURNED - 1:
+                turn_masters(i, ["bank_e0", "bank_e1", "bank_t0", "bank_t1"], nc.scalar.copy)
+            if i >= TURNED:
+                round_page(i, T2 // 2, T2)
             if b > 0 and c == 0:
-                finish_masters(b - 1, 0, "bank_w", nc.scalar.copy)
-                finish_masters(b - 1, 1, "bank_t1", nc.scalar.copy)
+                finish_masters(b - 1, 0, "bank_w0", nc.scalar.copy)
+                finish_masters(b - 1, 1, "bank_w1", nc.scalar.copy)
                 quantise_x(b - 1)
-            first = 2 * (c - 1) if b < last else 2 * c
-            if b > 0 and 0 <= first < 4:
-                for n, tag in ((first, "bank_w"), (first + 1, "bank_t1")):
-                    finish_page(b - 1, n, tag, nc.scalar.copy)
-                    quantise_page(b - 1, n)
-            if i + 5 < SLICES:
-                round_w1(i + 5)
-            if i == 7:
-                for m in range(3):
-                    scores(m, 0)
-            if i == SLICES - 2:
-                for m in range(3):
-                    scores(m, 1)
-                for m in range(3, 5):
-                    for bb in range(last):
-                        scores(m, bb)
-            if i == 3:
-                load_page(SLICES - 1)
+            for n in page_parts.get(i, ()):
+                finish_page(b - 1, n, ("bank_w0", "bank_w1")[n % 2] if b < last else e_banks[n], nc.scalar.copy)
+                quantise_page(b - 1, n)
+            if i + 4 < TURNED:
+                round_w1(i + 4)
+            if 1 <= i < 5:
+                round_w1_dealt(i - 1)
 
+        for m in range(MT):
+            for b in range(last):
+                scores(m, b)
         i = SLICES - 1
         scatter(i)
-        turn_page(i, ["bank_t0", "bank_t1"])
+        round_page(i, 0, 2 * P)
+        weave_page(0)
         gather(i)
-        xb[i] = ring.tile([P, NP], BF16, name="xb", bufs=2)
-        nc.vector.tensor_scalar(
-            xb[i][:], picked[i][:], chan[:, i : i + 1], chan[:, VEC_ROW + i : VEC_ROW + i + 1], ALU.subtract, ALU.mult
-        )
-        finish_page(last, 0, "bank_w", nc.scalar.copy)
-        turn_masters(i, "bank_t0", nc.vector.tensor_copy)
-        finish_page(last, 1, "bank_t1", nc.scalar.copy)
-        finish_masters(last, 0, "bank_w", nc.scalar.copy)
-        finish_masters(last, 1, "bank_t0", nc.vector.tensor_copy)
+        nc.vector.tensor_scalar(x_d[:, :, 3], picked[i][:], cen_d[:, 3:4], vec_d[:, 3:4], ALU.subtract, ALU.mult)
         quantise_page(last, 0)
         quantise_x(last)
-        finish_page(last, 2, "bank_t1", nc.scalar.copy)
-        finish_page(last, 3, "bank_w", nc.scalar.copy)
+        for n in range(1, 4):
+            round_page(i, 2 * P * n, 2 * P * (n + 1))
+            weave_page(n)
         for m in range(MT):
             if m % 2 == 1 and m < MT - 1:
                 quantise_page(last, (m + 1) // 2)
-            if m >= 5:
-                for bb in range(last):
-                    scores(m, bb)
             scores(m, last)
             weigh(m)

from contextlib import ExitStack

import concourse.mybir as mybir

F32 = mybir.dt.float32
BF16 = mybir.dt.bfloat16
I32 = mybir.dt.int32
U32 = mybir.dt.uint32
U16 = mybir.dt.uint16
U8 = mybir.dt.uint8
FP8X4 = mybir.dt.float8_e4m3fn_x4
FP4X4 = mybir.dt.float4_e2m1fn_x4
ALU = mybir.AluOpType
ACT = mybir.ActivationFunctionType

K, H, T, S, T2, NP = 1024, 1536, 2048, 512, 1024, 512
P = 128
KP = K // 512
RP = H // 512
SLICES = H // P
MT = T2 // P
TURNED = SLICES - 4
W1_CHUNKS = [(c, 1) for c in range(4)] + [(c, 2) for c in range(4, TURNED, 2)]
VEC_ROW = 32
FLOPS = 2 * (2 * K * H * S + H * T2 * NP)


def tile_list_diamond_master_compare_kernel(
    tc, tab_words, tab_scales, offs, w1, w4_words, w4_scales, res, page0, wgs, offs2, offs3, cen, vec, mat, out
):
    nc = tc.nc
    with ExitStack() as ctx:
        lists = ctx.enter_context(tc.tile_pool(name="lists", bufs=1))
        first = ctx.enter_context(tc.tile_pool(name="first", bufs=1))
        psum = ctx.enter_context(tc.psum_pool(name="psum", bufs=1))

        idx = lists.tile([P, S // 16], U16, name="idx")
        idx2 = lists.tile([P, S // 16], U16, name="idx2")
        idx3 = lists.tile([P, NP // 16], U16, name="idx3")

        tab_w, mat_t = {}, {}
        tab_w[0] = first.tile([P, T], I32, name="tab_w0", tag="big0")
        tab_s = first.tile([P, KP, T], U8, name="tab_s", tag="v_w1", align_bytes=64)
        warm = first.tile([P, 8], F32, name="warm")
        ident32 = first.tile([P, P], F32, name="ident32")
        ident16 = first.tile([P, P], BF16, name="ident16")

        def load_table(a):
            nc.sync.dma_start(tab_w[a][:], tab_words[a].rearrange("p n t -> p (n t)").bitcast(I32))

        def load_scale_rows(tile, scale_rows):
            for q in range(4):
                src = scale_rows[:, 4 * q : 4 * q + 4, :].rearrange("a r c -> r a c")
                nc.sync.dma_start(tile[32 * q : 32 * q + 4].bitcast(I32), src.bitcast(I32))

        nc.sync.dma_start(idx[:], offs)
        load_table(0)
        nc.vector.memset(tab_s[:].bitcast(I32), 0)
        load_scale_rows(tab_s, tab_scales)
        with tc.tile_pool(name="scratch", bufs=1) as scratch:
            ones = scratch.tile([P, P], F32, name="ones")
            nc.vector.memset(ones[:], 1.0)
            nc.gpsimd.affine_select(
                out=ident32[:], in_=ones[:], compare_op=ALU.is_equal, fill=0.0, base=0,
                pattern=[[-1, P]], channel_multiplier=1,
            )

        keep = ctx.enter_context(tc.tile_pool(name="keep", bufs=1))
        tab_w[1] = keep.tile([P, T], I32, name="tab_w1", tag="big1")
        v_w = {}
        v_s = [keep.tile([P, S], U8, name="v_s%d" % a, align_bytes=64) for a in range(KP)]
        w4_w = [keep.tile([P, KP, 1024], U8, name="w4_w%d" % b, align_bytes=64) for b in range(RP)]
        w4_s = keep.tile([P, KP, H], U8, name="w4_s", align_bytes=64)
        wg = keep.tile([P, S], F32, name="wg")
        rows = keep.tile([P, P], F32, name="rows")
        chan = keep.tile([P, 2 * VEC_ROW], F32, name="chan")
        shift = keep.tile([P, TURNED], F32, name="shift")
        raw_d = keep.tile([P, KP, 4, 512], F32, name="raw_d", align_bytes=64)
        dealt, top = {}, {}
        wg_d = keep.tile([P, 4, S], F32, name="wg_d")
        cen_d = keep.tile([P, 4], F32, name="cen_d")
        vec_d = keep.tile([P, 4], F32, name="vec_d")
        shift_d = keep.tile([P, 4], F32, name="shift_d")
        x_d = keep.tile([P, NP, 4], BF16, name="x_d", align_bytes=64)
        pg_w = [keep.tile([P, T2], U32, name="pg_w%d" % b, align_bytes=64) for b in range(RP)]
        pg_s = [keep.tile([P, T2], U8, name="pg_s%d" % b, align_bytes=64) for b in range(RP)]
        x_w = [keep.tile([P, NP], U32, name="x_w%d" % b, align_bytes=64) for b in range(RP)]
        x_s = [keep.tile([P, NP], U8, name="x_s%d" % b, align_bytes=64) for b in range(RP)]

        w1_raw, w1_grp, w1_w, w1_s = {}, {}, {}, {}
        res_t, page, hs, a1_ps, a2_ps, a2_sb, picked, xb = {}, {}, {}, {}, {}, {}, {}, {}
        pg_t, x_t, x_grp, pg_grp, e_ps, pairs = {}, {}, {}, {}, {}, {}

        def load_w1(n):
            first, count = W1_CHUNKS[n]
            raw = keep.tile([P, KP, 4, P * count], F32, name="w1_raw%d" % n, tag="raw%d" % n, align_bytes=64)
            for a in range(KP):
                src = w1[512 * a : 512 * (a + 1), P * first : P * (first + count)]
                nc.sync.dma_start(raw[:, a], src.rearrange("(p j) c -> p j c", j=4))
            for s in range(count):
                w1_raw[first + s] = raw[:, :, :, P * s : P * (s + 1)]

        def rows_of(i):
            if i < TURNED:
                return slice(P * i, P * (i + 1))
            return slice(P * TURNED + i - TURNED, H, 4)

        def load_w1_dealt(a):
            src = w1[512 * a : 512 * (a + 1), P * TURNED :]
            nc.sync.dma_start(raw_d[:, a], src.rearrange("(p j) c -> p j c", j=4))

        def load_w4(b):
            src = w4_words[:, :, 1024 * b : 1024 * (b + 1)].rearrange("a p c -> p a c")
            nc.sync.dma_start(w4_w[b][:].bitcast(I32), src.bitcast(I32))

        def load_res(i):
            res_t[i] = keep.tile([P, S], F32, name="res_t", tag="res%d" % i, align_bytes=64)
            nc.sync.dma_start(res_t[i][:], res[rows_of(i), :])

        def load_page(i):
            page[i] = keep.tile([P, T2], F32, name="page", bufs=8)
            nc.sync.dma_start(page[i][:], page0[rows_of(i), :])

        def load_mat(u):
            mat_t[u] = (first, keep)[u].tile([P, MT // 2, NP], F32, name="mat_t%d" % u, tag="big%d" % u)
            nc.sync.dma_start(mat_t[u][:], mat[512 * u : 512 * (u + 1), :].rearrange("(c p) j -> p c j", p=P))

        def round_w1(i, parts=1):
            tag = "w1q%d" % ((i - 2) % 3) if i > 0 else "grp0"
            grp = keep.tile([P, KP, P, 4], BF16, name="w1_grp", tag=tag, align_bytes=64)
            w1_grp[i] = grp[:]
            for a0 in range(0, KP, KP // parts):
                passes = slice(a0, a0 + KP // parts)
                nc.scalar.copy(
                    w1_grp[i][:, passes].rearrange("p a (c e) j -> p a c j e", e=4),
                    w1_raw[i][:, passes].rearrange("p a j (c e) -> p a c j e", e=4),
                )

        def round_w1_dealt(n):
            a, half = divmod(n, 2)
            if n == 0:
                dealt["w1"] = keep.tile([P, 4, KP, P, 4], BF16, name="grp_d", tag="raw4", align_bytes=64)
            nc.scalar.copy(
                dealt["w1"][:, :, a, 64 * half : 64 * (half + 1), :].rearrange("p t q j -> p q j t"),
                raw_d[:, a, :, 256 * half : 256 * (half + 1)].rearrange("p j (q t) -> p q j t", t=4),
            )

        def deal_w4_words():
            dealt["words"] = keep.tile([P, 4, KP, 2 * P], U8, name="w4_wd", tag="grp0", align_bytes=64)
            last_block = w4_w[RP - 1][:].bitcast(U16).rearrange("p a (q t) -> p t a q", t=4)
            nc.vector.tensor_copy(dealt["words"][:].bitcast(U16), last_block)

        def deal_w4_scales():
            dealt["scales"] = keep.tile([P, 4, KP, P], U8, name="w4_sd", tag="raw0", align_bytes=64)
            last_block = w4_s[:, :, P * TURNED :].rearrange("p a (q t) -> p t a q", t=4)
            nc.vector.tensor_copy(dealt["scales"][:], last_block)

        def quantise_w1(i, parts=1):
            plane_tag = "w1_s%d" % i if i < 2 else "res%d" % (i - 1 if i < 4 else i - 2)
            w1_w[i] = keep.tile([P, KP, P], U32, name="w1_w", tag="w1q%d" % (i % 3), align_bytes=64)
            w1_s[i] = keep.tile([P, KP, P], U8, name="w1_s", tag=plane_tag, align_bytes=64)
            if i >= TURNED:
                w1_grp[i] = dealt["w1"][:, i - TURNED]
            for a0 in range(0, KP, KP // parts):
                passes = slice(a0, a0 + KP // parts)
                nc.vector.quantize_mx(
                    w1_w[i][:, passes].rearrange("p a c -> p (a c)").bitcast(FP8X4),
                    w1_s[i][:, passes].rearrange("p a c -> p (a c)"),
                    w1_grp[i][:, passes].rearrange("p a c j -> p (a c j)"),
                )

        def reading_w1(i):
            a1_ps[i] = psum.tile([P, S], F32, name="a1", tag="bank_a1")
            for a in range(KP):
                nc.tensor.matmul_mx(
                    a1_ps[i][:], lhsT=w1_w[i][:, a].bitcast(FP8X4), lhsT_scale=w1_s[i][:, a],
                    rhs=v_w[a][:].bitcast(FP8X4), rhs_scale=v_s[a][:], start=a == 0, stop=a == KP - 1,
                )

        def reading_w4(i):
            b, c = divmod(i, 4)
            a2_ps[i] = psum.tile([P, S], F32, name="a2", tag="bank_a2")
            for a in range(KP):
                if i < TURNED:
                    words, scales = w4_w[b][:, a, 2 * P * c : 2 * P * (c + 1)], w4_s[:, a, P * i : P * (i + 1)]
                else:
                    words, scales = dealt["words"][:, c, a], dealt["scales"][:, c, a]
                nc.tensor.matmul_mx(
                    a2_ps[i][:], lhsT=words.bitcast(FP4X4), lhsT_scale=scales,
                    rhs=v_w[a][:].bitcast(FP8X4), rhs_scale=v_s[a][:], start=a == 0, stop=a == KP - 1,
                )

        def fetch_w4(i):
            a2_sb[i] = keep.tile([P, S], F32, name="a2_sb", tag="raw1" if i > 0 else "raw0", align_bytes=64)
            nc.scalar.copy(a2_sb[i][:], a2_ps[i][:])

        def larger(i):
            top[i] = keep.tile([P, S], F32, name="top", tag="top" if i != 1 else "h0")
            nc.vector.tensor_tensor(top[i][:], a1_ps[i][:], a2_sb[i][:], ALU.max)

        def residual(i):
            hs[i] = keep.tile([P, S], F32, name="h", tag="h%d" % (i % 2))
            engine = nc.gpsimd if i > 0 else nc.vector
            engine.tensor_tensor(hs[i][:], top[i][:], res_t[i][:], ALU.subtract)

        def scatter(i):
            nc.vector.tensor_tensor(page[i][:].indirect(idx2[:]), hs[i][:], wg[:] if i < TURNED else wg_d[:, i - TURNED], ALU.mult)

        def gather(i):
            picked[i] = keep.tile([P, NP], F32, name="picked", tag="raw1", align_bytes=64)
            nc.vector.tensor_copy(picked[i][:], page[i][:].indirect(idx3[:]))

        def turn_page(i, tags):
            b, c = divmod(i, 4)
            for half in range(2):
                if c == 0:
                    tag = "raw2" if (b, half) == (0, 0) else "pg_t%d%d" % (b, half)
                    pg_t[b, half] = keep.tile([P, 4, 2, 2 * P], BF16, name="pg_t", tag=tag, align_bytes=64)
                bank = psum.tile([P, 4, P], F32, name="turn", tag=tags[half])
                for g in range(4):
                    m0 = P * (4 * half + g)
                    nc.tensor.transpose(bank[:, g, :], page[i][:, m0 : m0 + P], ident32[:])
                nc.scalar.copy(
                    pg_t[b, half][:, :, :, 64 * c : 64 * (c + 1)].rearrange("m g u (q e) -> m g u q e", e=2),
                    bank[:].rearrange("m g (q u e) -> m g u q e", u=2, e=2),
                )

        def negated_product(dst, left, right):
            nc.gpsimd.tensor_tensor(dst, left, right, ALU.mult)
            nc.gpsimd.tensor_scalar(dst, dst, -1.0, 0.0, ALU.mult, ALU.add)

        def centre(i):
            if i < TURNED - 1:
                xb[i] = keep.tile([P, NP], BF16, name="xb", bufs=2)
            else:
                xb[i] = keep.tile([P, NP], BF16, name="xb_last", tag="raw5", align_bytes=64)
            nc.scalar.activation(
                xb[i][:], picked[i][:], ACT.Identity, bias=shift[:, i : i + 1],
                scale=chan[:, VEC_ROW + i : VEC_ROW + i + 1],
            )

        def round_page(i, c0, c1):
            u, e = divmod(i - TURNED, 2)
            nc.scalar.copy(pairs[0][:, u, c0:c1, e], page[i][:, c0:c1])

        def weave_page(n):
            pg_grp[RP - 1, n] = keep.tile([P, 2 * P, 2], F32, name="pg_grp", bufs=4, align_bytes=64)
            words = pairs[0][:].rearrange("p u m e -> p u (m e)").bitcast(F32)
            nc.scalar.copy(pg_grp[RP - 1, n][:], words[:, :, 2 * P * n : 2 * P * (n + 1)].rearrange("p u m -> p m u"))

        def centre_dealt(i):
            t = i - TURNED
            nc.scalar.activation(
                x_d[:, :, t], picked[i][:], ACT.Identity, bias=shift_d[:, t : t + 1], scale=vec_d[:, t : t + 1]
            )

        def turn_masters(i, tags, copy):
            b, c = divmod(i, 4)
            if c == 0:
                x_t[b] = keep.tile([P, 4, 2, P], F32, name="x_t", bufs=2)
            share = 4 // len(tags)
            for n, tag in enumerate(tags):
                bank = psum.tile([P, share, P], BF16, name="turn_x", tag=tag)
                for g in range(share):
                    j0 = P * (share * n + g)
                    nc.tensor.transpose(bank[:, g, :], xb[i][:, j0 : j0 + P], ident16[:])
                copy(
                    x_t[b][:, share * n : share * (n + 1), :, 32 * c : 32 * (c + 1)],
                    bank[:].bitcast(F32).rearrange("j g (q u) -> j g u q", u=2),
                )

        def turn_back(words, dst, tag, copy):
            bank = psum.tile([P, 2, 2, P], F32, name="back", tag=tag)
            for g in range(2):
                for u in range(2):
                    nc.tensor.transpose(bank[:, g, u, :], words[:, g, u, :], ident32[:])
            copy(dst.rearrange("p (g m) u -> p g m u", g=2), bank[:].rearrange("p g u m -> p g m u"))

        def finish_masters(b, n, tag, copy):
            if n == 0:
                x_grp[b] = keep.tile([P, NP, 2], F32, name="x_grp", bufs=1, align_bytes=64)
            turn_back(x_t[b][:, 2 * n : 2 * n + 2], x_grp[b][:, 2 * P * n : 2 * P * (n + 1), :], tag, copy)

        def quantise_x(b):
            if b < RP - 1:
                src = x_grp[b][:].rearrange("p n u -> p (n u)").bitcast(BF16)
            else:
                src = x_d[:].rearrange("p n t -> p (n t)")
            nc.vector.quantize_mx(x_w[b][:].bitcast(FP8X4), x_s[b][:], src)

        def finish_page(b, n, tag, copy):
            pg_grp[b, n] = keep.tile([P, 2 * P, 2], F32, name="pg_grp", bufs=4, align_bytes=64)
            words = pg_t[b, n // 2][:].bitcast(F32)
            turn_back(words[:, 2 * (n % 2) : 2 * (n % 2) + 2], pg_grp[b, n][:], tag, copy)

        def quantise_page(b, n):
            cols = slice(2 * P * n, 2 * P * (n + 1))
            src = pg_grp[b, n][:].rearrange("p m u -> p (m u)").bitcast(BF16)
            nc.vector.quantize_mx(pg_w[b][:, cols].bitcast(FP8X4), pg_s[b][:, cols], src)

        e_banks = ["bank_e0", "bank_e1", "bank_t0", "bank_t1", "bank_a2", "bank_a1", "bank_w0", "bank_w1"]

        def scores(m, b):
            if b == 0:
                e_ps[m] = psum.tile([P, NP], F32, name="e_ps", tag=e_banks[m])
            cols = slice(P * m, P * (m + 1))
            nc.tensor.matmul_mx(
                e_ps[m][:], lhsT=pg_w[b][:, cols].bitcast(FP8X4), lhsT_scale=pg_s[b][:, cols],
                rhs=x_w[b][:].bitcast(FP8X4), rhs_scale=x_s[b][:], start=b == 0, stop=b == RP - 1,
            )

        result_tags = ["res%d" % m for m in range(MT)]

        def weigh(m):
            result = keep.tile([P, NP], F32, name="result", tag=result_tags[m], align_bytes=64)
            nc.vector.tensor_tensor(result[:], e_ps[m][:], mat_t[m // 4][:, m % 4, :], ALU.mult)
            nc.sync.dma_start(out[P * m : P * (m + 1), :], result[:])

        nc.vector.memset(warm[:], 0.0)
        nc.scalar.activation(warm[:, 0:1], warm[:, 1:2], ACT.Identity, bias=warm[:, 2:3], scale=warm[:, 3:4])
        nc.gpsimd.memset(w4_s[:].bitcast(I32), 0)
        nc.gpsimd.memset(rows[:], 0.0)
        nc.gpsimd.tensor_copy(ident16[:], ident32[:])

        load_table(1)
        load_w4(0)
        load_scale_rows(w4_s, w4_scales)
        load_w4(RP - 1)
        load_w1(0)
        load_w1(1)
        nc.sync.dma_start(wg[:], wgs)
        nc.sync.dma_start(idx2[:], offs2)
        load_page(0)
        load_res(0)
        load_w1(2)
        nc.sync.dma_start(idx3[:], offs3)
        nc.sync.dma_start(rows[0:TURNED, :], cen[: P * TURNED].rearrange("(c p) -> c p", p=P))
        nc.sync.dma_start(rows[VEC_ROW : VEC_ROW + TURNED, :], vec[: P * TURNED].rearrange("(c p) -> c p", p=P))
        nc.sync.dma_start(cen_d[:], cen[P * TURNED :].rearrange("(p t) -> p t", t=4))
        nc.sync.dma_start(vec_d[:], vec[P * TURNED :].rearrange("(p t) -> p t", t=4))
        w1_before = {1: (3, 4), 2: (5,)}
        for i in range(1, SLICES):
            for n in w1_before.get(i, ()):
                load_w1(n)
            if i == 2:
                load_w4(1)
            if 0 <= i - 3 < KP:
                load_w1_dealt(i - 3)
            if i == TURNED:
                for u in range(4):
                    nc.sync.dma_start(wg_d[32 * u : 32 * (u + 1)], wgs.rearrange("(q t) j -> q t j", t=4))
            load_page(i)
            load_res(i)
        for u in range(2):
            load_mat(u)

        for a in range(KP):
            nc.vector.tensor_copy(v_s[a][:], tab_s[:, a, :].indirect(idx[:]))
        for a in range(KP):
            v_w[a] = first.tile([P, S], U32, name="v_w%d" % a, tag="v_w%d" % a, align_bytes=64)
            nc.vector.tensor_copy(v_w[a][:], tab_w[a][:].bitcast(U32).indirect(idx[:]))
        reading_w4(0)
        round_w1(0, KP)
        quantise_w1(0, KP)
        fetch_w4(0)
        reading_w1(0)
        deal_w4_words()
        round_w1(1)
        larger(0)
        deal_w4_scales()
        reading_w4(1)
        quantise_w1(1)
        residual(0)
        fetch_w4(1)
        reading_w1(1)
        reading_w4(2)
        turned = psum.tile([P, P], F32, name="turned", tag="bank_w0")
        nc.tensor.transpose(turned[:], rows[:], ident32[:])
        nc.scalar.copy(chan[:], turned[:, 0 : 2 * VEC_ROW])
        round_w1(2)
        negated_product(shift[:], chan[:, 0:TURNED], chan[:, VEC_ROW : VEC_ROW + TURNED])
        round_w1(3)

        negated_product(shift_d[:], cen_d[:], vec_d[:])

        last = RP - 1
        page_parts = {5: (0, 1), 6: (2, 3), 8: (0,), 9: (1, 2, 3)}
        for i in range(SLICES - 1):
            b, c = divmod(i, 4)
            scatter(i)
            larger(i + 1)
            if 2 <= i < SLICES - 2:
                reading_w1(i + 2)
            if i < TURNED:
                turn_page(i, ["bank_t0", "bank_t1"])
            else:
                if i == TURNED:
                    pairs[0] = keep.tile([P, 2, T2, 2], BF16, name="pairs", tag="raw5", align_bytes=64)
                round_page(i, 0, T2 // 2)
            gather(i)
            residual(i + 1)
            if i < 2:
                quantise_w1(i + 2)
                reading_w1(i + 2)
            if 1 <= i < SLICES - 3:
                quantise_w1(i + 3)
            if i < TURNED:
                centre(i)
            else:
                centre_dealt(i)
            if i + 2 < SLICES:
                fetch_w4(i + 2)
            if i + 3 < SLICES:
                reading_w4(i + 3)
            if i < TURNED - 1:
                turn_masters(i, ["bank_t0", "bank_t1"], nc.scalar.copy)
            if i == TURNED - 1:
                turn_masters(i, ["bank_e0", "bank_e1", "bank_t0", "bank_t1"], nc.scalar.copy)
            if i >= TURNED:
                round_page(i, T2 // 2, T2)
            if b > 0 and c == 0:
                finish_masters(b - 1, 0, "bank_w0", nc.scalar.copy)
                finish_masters(b - 1, 1, "bank_w1", nc.scalar.copy)
                quantise_x(b - 1)
            for n in page_parts.get(i, ()):
                finish_page(b - 1, n, ("bank_w0", "bank_w1")[n % 2] if b < last else e_banks[n], nc.scalar.copy)
                quantise_page(b - 1, n)
            if i + 4 < TURNED:
                round_w1(i + 4)
            if 1 <= i < 5:
                round_w1_dealt(i - 1)

        for m in range(MT):
            for b in range(last):
                scores(m, b)
        i = SLICES - 1
        scatter(i)
        round_page(i, 0, 2 * P)
        weave_page(0)
        gather(i)
        nc.vector.tensor_scalar(x_d[:, :, 3], picked[i][:], cen_d[:, 3:4], vec_d[:, 3:4], ALU.subtract, ALU.mult)
        quantise_page(last, 0)
        quantise_x(last)
        for n in range(1, 4):
            round_page(i, 2 * P * n, 2 * P * (n + 1))
            weave_page(n)
        for m in range(MT):
            if m % 2 == 1 and m < MT - 1:
                quantise_page(last, (m + 1) // 2)
            scores(m, last)
            weigh(m)
